import numpy as np
import ml_dtypes


def mxq(x, axis, fmt="e4m3"):
    dtype, down = {"e4m3": (ml_dtypes.float8_e4m3fn, 7), "e5m2": (ml_dtypes.float8_e5m2, 14)}[fmt]
    v = np.moveaxis(np.asarray(x, np.float32).astype(ml_dtypes.bfloat16).astype(np.float64), axis, -1)
    blocks = v.reshape(v.shape[:-1] + (-1, 32))
    amax = np.abs(blocks).max(-1, keepdims=True)
    byte = np.maximum(np.where(amax > 0, np.frexp(amax)[1] - 1 + 127, 0) - down, 1)
    scale = np.exp2(byte - 127.0)
    codes = (blocks / scale).astype(np.float32).astype(dtype).astype(np.float64)
    return np.moveaxis((codes * scale).reshape(v.shape), -1, axis)


WIDE = False


def mx_kscale(k):
    if not WIDE:
        return np.ones(k)
    levels = np.array([10, -10, 5, -5, 0])
    if k % 512:
        return np.exp2(np.random.permutation(np.resize(levels, k // 32))).repeat(32)
    a = np.empty((k // 512, 16))
    for p in range(k // 512):
        a[p, :8] = np.random.permutation(np.resize(levels, 8))
        for g in range(8):
            far = levels[np.abs(levels - a[p, g]) >= 10]
            a[p, g + 8] = far[np.random.randint(len(far))]
    return np.exp2(a.ravel()).repeat(32)


def f64(x):
    return np.asarray(x).astype(np.float64)


def striped(idx):
    return np.tile(idx.reshape(-1, 16).T, (8, 1)).astype(np.uint16)


def unstriped(offs):
    return offs[:16].T.reshape(-1).astype(np.int64)


def gelu(v):
    return 0.5 * v * (1.0 + np.tanh(np.sqrt(2.0 / np.pi) * (v + 0.044715 * v**3)))


K, T, S, N = 512, 256, 512, 2048


def setup_inputs():
    n = np.random.standard_normal
    s = mx_kscale(K)[:, None]
    return {
        "w": (n((K, N)) / np.sqrt(K) / s).astype(np.float32),
        "xT": (n((K, T)) * s).astype(np.float32),
        "b": (0.3 * n((S, 1))).astype(np.float32),
        "offs": striped(np.sort(np.random.permutation(N)[:S])),
    }


def reference(w, xT, b, offs):
    idx = unstriped(offs)
    wq = mxq(f64(w)[:, idx], 0, "e4m3")
    return gelu((wq.T @ mxq(f64(xT), 0, "e4m3")) + f64(b))

@@ -1,0 +1,101 @@
+from contextlib import ExitStack
+
+import concourse.mybir as mybir
+from concourse.masks import make_identity
+
+K, N, S, T = 512, 2048, 512, 256
+FLOPS = 2 * K * S * T
+
+F32 = mybir.dt.float32
+BF16 = mybir.dt.bfloat16
+U32 = mybir.dt.uint32
+U16 = mybir.dt.uint16
+U8 = mybir.dt.uint8
+FP8X4 = mybir.dt.float8_e4m3fn_x4
+ACT = mybir.ActivationFunctionType
+
+P = 128
+PACK = 4
+HALF = S // 2
+M_TILES = S // P
+
+
+def tile_picked_neuron_lin_gelu_srt_e_kernel(tc, w, xT, b, offs, out):
+    nc = tc.nc
+    with ExitStack() as ctx:
+        keep = ctx.enter_context(tc.tile_pool(name="keep", bufs=1))
+        psum = ctx.enter_context(tc.psum_pool(name="psum", bufs=1))
+
+        offsets = keep.tile([P, S // 16], U16, name="offsets")
+        nc.sync.dma_start(offsets[:], offs)
+        w_rows = w.rearrange("(p j) n -> p j n", j=PACK)
+        planes = []
+        for j in range(PACK):
+            plane = keep.tile([P, N], F32, name=f"plane{j}", align_bytes=64)
+            nc.sync.dma_start(out=plane[:], in_=w_rows[:, j, :])
+            planes.append(plane)
+        x_raw = keep.tile([P, PACK, T], F32, name="x_raw", align_bytes=64)
+        nc.sync.dma_start(out=x_raw[:], in_=xT.rearrange("(p j) t -> p j t", j=PACK))
+
+        b_rows = keep.tile([P, P], F32, name="b_rows", align_bytes=64)
+        nc.vector.memset(b_rows[:], 0.0)
+        warm = keep.tile([P, 1], F32, name="warm")
+        nc.vector.memset(warm[:], 0.0)
+        nc.scalar.dma_start(out=b_rows[0:M_TILES, :], in_=b.rearrange("(m p) o -> m (p o)", p=P))
+        ident = keep.tile([P, P], F32, name="ident", align_bytes=64)
+        make_identity(nc, ident[:])
+        table = keep.tile([P, 1], F32, name="table")
+        nc.scalar.activation(out=table[:], in_=warm[:], func=ACT.Gelu_apprx_tanh)
+        b_turned = psum.tile([P, P], F32, name="b_turned")
+        nc.tensor.transpose(b_turned[:], b_rows[:], ident[:])
+        bias = keep.tile([P, M_TILES], F32, name="bias")
+        nc.scalar.copy(out=bias[:], in_=b_turned[:, 0:M_TILES])
+
+        w_bf = keep.tile([P, S, PACK], BF16, name="w_bf", align_bytes=64)
+        for j in range(PACK - 1):
+            nc.vector.tensor_copy(out=w_bf[:, :, j], in_=planes[j][:].indirect(offsets[:]))
+        for h in range(2):
+            nc.vector.tensor_copy(
+                out=w_bf[:, h * HALF : (h + 1) * HALF, PACK - 1],
+                in_=planes[PACK - 1][:].indirect(offsets[:, h * HALF // 16 : (h + 1) * HALF // 16]),
+            )
+
+        x_bf = keep.tile([P, T, PACK], BF16, name="x_bf", align_bytes=64)
+        for t0 in range(0, T, P):
+            nc.scalar.copy(out=x_bf[:, t0 : t0 + P, :], in_=x_raw[:, :, t0 : t0 + P].rearrange("p j t -> p t j"))
+
+        w_codes = keep.tile([P, S], U32, name="w_codes", align_bytes=64)
+        w_scales = keep.tile([P, S], U8, name="w_scales", align_bytes=64)
+        x_codes = keep.tile([P, T], U32, name="x_codes", align_bytes=64)
+        x_scales = keep.tile([P, T], U8, name="x_scales", align_bytes=64)
+
+        def quantise(codes, scales, values, c0):
+            cols = slice(c0, c0 + P)
+            nc.vector.quantize_mx(
+                out=codes[:, cols].bitcast(FP8X4),
+                scales=scales[:, cols],
+                in_=values[:, cols, :].rearrange("p c j -> p (c j)"),
+            )
+
+        for c0 in range(0, HALF, P):
+            quantise(w_codes, w_scales, w_bf, c0)
+        for t0 in range(0, T, P):
+            quantise(x_codes, x_scales, x_bf, t0)
+        for c0 in range(HALF, S, P):
+            quantise(w_codes, w_scales, w_bf, c0)
+
+        for m in range(M_TILES):
+            cols = slice(m * P, (m + 1) * P)
+            acc = psum.tile([P, T], F32, name=f"acc{m}")
+            nc.tensor.matmul_mx(
+                out=acc[:],
+                lhsT=w_codes[:, cols].bitcast(FP8X4),
+                lhsT_scale=w_scales[:, cols],
+                rhs=x_codes[:].bitcast(FP8X4),
+                rhs_scale=x_scales[:],
+                start=True,
+                stop=True,
+            )
+            result = keep.tile([P, T], F32, name=f"result{m}", align_bytes=64)
+            nc.scalar.activation(out=result[:], in_=acc[:], func=ACT.Gelu_apprx_tanh, bias=bias[:, m : m + 1])
+            nc.sync.dma_start(out=out[cols, :], in_=result[:])

@@ -46,7 +46,7 @@ def tile_picked_neuron_lin_gelu_srt_e_kernel(tc, w, xT, b, offs, out):
         make_identity(nc, ident[:])
         table = keep.tile([P, 1], F32, name="table")
         nc.scalar.activation(out=table[:], in_=warm[:], func=ACT.Gelu_apprx_tanh)
-        b_turned = psum.tile([P, P], F32, name="b_turned")
+        b_turned = psum.tile([P, P], F32, name="b_turned", tag="bank3_128")
         nc.tensor.transpose(b_turned[:], b_rows[:], ident[:])
         bias = keep.tile([P, M_TILES], F32, name="bias")
         nc.scalar.copy(out=bias[:], in_=b_turned[:, 0:M_TILES])
@@ -77,25 +77,29 @@ def tile_picked_neuron_lin_gelu_srt_e_kernel(tc, w, xT, b, offs, out):
                 in_=values[:, cols, :].rearrange("p c j -> p (c j)"),
             )
 
-        for c0 in range(0, HALF, P):
+        quantise(w_codes, w_scales, w_bf, 0)
+        quantise(x_codes, x_scales, x_bf, 0)
+        for c0 in range(P, S, P):
             quantise(w_codes, w_scales, w_bf, c0)
-        for t0 in range(0, T, P):
-            quantise(x_codes, x_scales, x_bf, t0)
-        for c0 in range(HALF, S, P):
-            quantise(w_codes, w_scales, w_bf, c0)
+        quantise(x_codes, x_scales, x_bf, P)
 
-        for m in range(M_TILES):
-            cols = slice(m * P, (m + 1) * P)
-            acc = psum.tile([P, T], F32, name=f"acc{m}")
-            nc.tensor.matmul_mx(
-                out=acc[:],
-                lhsT=w_codes[:, cols].bitcast(FP8X4),
-                lhsT_scale=w_scales[:, cols],
-                rhs=x_codes[:].bitcast(FP8X4),
-                rhs_scale=x_scales[:],
-                start=True,
-                stop=True,
-            )
-            result = keep.tile([P, T], F32, name=f"result{m}", align_bytes=64)
-            nc.scalar.activation(out=result[:], in_=acc[:], func=ACT.Gelu_apprx_tanh, bias=bias[:, m : m + 1])
-            nc.sync.dma_start(out=out[cols, :], in_=result[:])
+        results = [keep.tile([P, T], F32, name=f"result{m}", align_bytes=64) for m in range(M_TILES)]
+        for t0 in range(0, T, P):
+            tokens = slice(t0, t0 + P)
+            for m in range(M_TILES):
+                cols = slice(m * P, (m + 1) * P)
+                acc = psum.tile([P, P], F32, name=f"acc{m}_{t0}", tag=f"bank{m}_{t0}")
+                nc.tensor.matmul_mx(
+                    out=acc[:],
+                    lhsT=w_codes[:, cols].bitcast(FP8X4),
+                    lhsT_scale=w_scales[:, cols],
+                    rhs=x_codes[:, tokens].bitcast(FP8X4),
+                    rhs_scale=x_scales[:, tokens],
+                    start=True,
+                    stop=True,
+                )
+                nc.scalar.activation(
+                    out=results[m][:, tokens], in_=acc[:], func=ACT.Gelu_apprx_tanh, bias=bias[:, m : m + 1]
+                )
+                if t0 + P == T:
+                    nc.sync.dma_start(out=out[cols, :], in_=results[m][:])

from contextlib import ExitStack

import concourse.mybir as mybir
from concourse.masks import make_identity

K, N, S, T = 512, 2048, 512, 256
FLOPS = 2 * K * S * T

F32 = mybir.dt.float32
BF16 = mybir.dt.bfloat16
U32 = mybir.dt.uint32
U16 = mybir.dt.uint16
U8 = mybir.dt.uint8
FP8X4 = mybir.dt.float8_e4m3fn_x4
ACT = mybir.ActivationFunctionType

P = 128
PACK = 4
HALF = S // 2
M_TILES = S // P


def tile_picked_neuron_lin_gelu_srt_e_kernel(tc, w, xT, b, offs, out):
    nc = tc.nc
    with ExitStack() as ctx:
        keep = ctx.enter_context(tc.tile_pool(name="keep", bufs=1))
        psum = ctx.enter_context(tc.psum_pool(name="psum", bufs=1))

        offsets = keep.tile([P, S // 16], U16, name="offsets")
        nc.sync.dma_start(offsets[:], offs)
        w_rows = w.rearrange("(p j) n -> p j n", j=PACK)
        planes = []
        for j in range(PACK):
            plane = keep.tile([P, N], F32, name=f"plane{j}", align_bytes=64)
            nc.sync.dma_start(out=plane[:], in_=w_rows[:, j, :])
            planes.append(plane)
        x_raw = keep.tile([P, PACK, T], F32, name="x_raw", align_bytes=64)
        nc.sync.dma_start(out=x_raw[:], in_=xT.rearrange("(p j) t -> p j t", j=PACK))

        b_rows = keep.tile([P, P], F32, name="b_rows", align_bytes=64)
        nc.vector.memset(b_rows[:], 0.0)
        warm = keep.tile([P, 1], F32, name="warm")
        nc.vector.memset(warm[:], 0.0)
        nc.scalar.dma_start(out=b_rows[0:M_TILES, :], in_=b.rearrange("(m p) o -> m (p o)", p=P))
        ident = keep.tile([P, P], F32, name="ident", align_bytes=64)
        make_identity(nc, ident[:])
        table = keep.tile([P, 1], F32, name="table")
        nc.scalar.activation(out=table[:], in_=warm[:], func=ACT.Gelu_apprx_tanh)
        b_turned = psum.tile([P, P], F32, name="b_turned", tag="bank3_128")
        nc.tensor.transpose(b_turned[:], b_rows[:], ident[:])
        bias = keep.tile([P, M_TILES], F32, name="bias")
        nc.scalar.copy(out=bias[:], in_=b_turned[:, 0:M_TILES])

        w_bf = keep.tile([P, S, PACK], BF16, name="w_bf", align_bytes=64)
        for j in range(PACK - 1):
            nc.vector.tensor_copy(out=w_bf[:, :, j], in_=planes[j][:].indirect(offsets[:]))
        for h in range(2):
            nc.vector.tensor_copy(
                out=w_bf[:, h * HALF : (h + 1) * HALF, PACK - 1],
                in_=planes[PACK - 1][:].indirect(offsets[:, h * HALF // 16 : (h + 1) * HALF // 16]),
            )

        x_bf = keep.tile([P, T, PACK], BF16, name="x_bf", align_bytes=64)
        for t0 in range(0, T, P):
            nc.scalar.copy(out=x_bf[:, t0 : t0 + P, :], in_=x_raw[:, :, t0 : t0 + P].rearrange("p j t -> p t j"))

        w_codes = keep.tile([P, S], U32, name="w_codes", align_bytes=64)
        w_scales = keep.tile([P, S], U8, name="w_scales", align_bytes=64)
        x_codes = keep.tile([P, T], U32, name="x_codes", align_bytes=64)
        x_scales = keep.tile([P, T], U8, name="x_scales", align_bytes=64)

        def quantise(codes, scales, values, c0):
            cols = slice(c0, c0 + P)
            nc.vector.quantize_mx(
                out=codes[:, cols].bitcast(FP8X4),
                scales=scales[:, cols],
                in_=values[:, cols, :].rearrange("p c j -> p (c j)"),
            )

        quantise(w_codes, w_scales, w_bf, 0)
        quantise(x_codes, x_scales, x_bf, 0)
        for c0 in range(P, S, P):
            quantise(w_codes, w_scales, w_bf, c0)
        quantise(x_codes, x_scales, x_bf, P)

        results = [keep.tile([P, T], F32, name=f"result{m}", align_bytes=64) for m in range(M_TILES)]
        for t0 in range(0, T, P):
            tokens = slice(t0, t0 + P)
            for m in range(M_TILES):
                cols = slice(m * P, (m + 1) * P)
                acc = psum.tile([P, P], F32, name=f"acc{m}_{t0}", tag=f"bank{m}_{t0}")
                nc.tensor.matmul_mx(
                    out=acc[:],
                    lhsT=w_codes[:, cols].bitcast(FP8X4),
                    lhsT_scale=w_scales[:, cols],
                    rhs=x_codes[:, tokens].bitcast(FP8X4),
                    rhs_scale=x_scales[:, tokens],
                    start=True,
                    stop=True,
                )
                nc.scalar.activation(
                    out=results[m][:, tokens], in_=acc[:], func=ACT.Gelu_apprx_tanh, bias=bias[:, m : m + 1]
                )
                if t0 + P == T:
                    nc.sync.dma_start(out=out[cols, :], in_=results[m][:])
